import numpy as np
import ml_dtypes


def mxq(x, axis, fmt="e4m3"):
    dtype, down = {"e4m3": (ml_dtypes.float8_e4m3fn, 7), "e5m2": (ml_dtypes.float8_e5m2, 14)}[fmt]
    v = np.moveaxis(np.asarray(x, np.float32).astype(ml_dtypes.bfloat16).astype(np.float64), axis, -1)
    blocks = v.reshape(v.shape[:-1] + (-1, 32))
    amax = np.abs(blocks).max(-1, keepdims=True)
    byte = np.maximum(np.where(amax > 0, np.frexp(amax)[1] - 1 + 127, 0) - down, 1)
    scale = np.exp2(byte - 127.0)
    codes = (blocks / scale).astype(np.float32).astype(dtype).astype(np.float64)
    return np.moveaxis((codes * scale).reshape(v.shape), -1, axis)


WIDE = False


def mx_kscale(k):
    if not WIDE:
        return np.ones(k)
    levels = np.array([10, -10, 5, -5, 0])
    if k % 512:
        return np.exp2(np.random.permutation(np.resize(levels, k // 32))).repeat(32)
    a = np.empty((k // 512, 16))
    for p in range(k // 512):
        a[p, :8] = np.random.permutation(np.resize(levels, 8))
        for g in range(8):
            far = levels[np.abs(levels - a[p, g]) >= 10]
            a[p, g + 8] = far[np.random.randint(len(far))]
    return np.exp2(a.ravel()).repeat(32)


def f64(x):
    return np.asarray(x).astype(np.float64)


def striped(idx):
    return np.tile(idx.reshape(-1, 16).T, (8, 1)).astype(np.uint16)


def unstriped(offs):
    return offs[:16].T.reshape(-1).astype(np.int64)


def striped8(idx):
    return np.concatenate([x.reshape(-1, 16).T for x in idx]).astype(np.uint16)


def runs(offs, k):
    lists = np.stack([offs[16 * r : 16 * r + 16].T.reshape(-1) for r in range(8)]).astype(np.int64)
    return lists[np.arange(k) % 512 // 64]


def pack_weight(w):
    k, n = w.shape
    w = f64(np.asarray(w, np.float32).astype(ml_dtypes.bfloat16)).reshape(k // 32, 32, n)
    amax = np.abs(w).max(1)
    byte = np.clip(np.where(amax > 0, np.frexp(amax)[1] - 1 + 127 - 7, 1), 1, 254)
    scaled = (w * np.exp2(127.0 - byte)[:, None, :]).reshape(k, n).astype(np.float32)
    words = np.ascontiguousarray(scaled.reshape(k // 512, 128, 4, n).transpose(0, 1, 3, 2)).astype(ml_dtypes.float8_e4m3fn).view(np.uint8)
    return words, np.ascontiguousarray(byte.astype(np.uint8).reshape(k // 512, 16, n))


def unpack_weight(words, scales):
    g, p, n, _ = words.shape
    vals = np.ascontiguousarray(words).view(ml_dtypes.float8_e4m3fn).astype(np.float64) * np.repeat(np.exp2(scales.astype(np.float64) - 127.0), 8, axis=1)[..., None]
    return vals.transpose(0, 1, 3, 2).reshape(g * 512, n)

def planes(y):
    n, m = y.shape
    v = y.astype(np.float32).astype(ml_dtypes.bfloat16).astype(np.float64).reshape(n // 32, 32, m)
    top = np.abs(v).max(1)
    byte = np.clip(np.where(top > 0, np.frexp(top)[1] - 1 + 127 - 7, 1), 1, 254)
    codes = (v * np.exp2(127.0 - byte)[:, None, :]).reshape(n, m).astype(np.float32).astype(ml_dtypes.float8_e4m3fn).view(np.uint8)
    words = codes.reshape(n // 512, 128, 4, m).transpose(0, 1, 3, 2)
    return np.ascontiguousarray(words), np.ascontiguousarray(byte.astype(np.uint8).reshape(n // 512, 16, m))


K, T, S, N, H, W = 512, 2048, 512, 512, 512, 2048


def setup_inputs():
    n = np.random.standard_normal
    s = mx_kscale(K)[:, None]
    u = mx_kscale(H)
    packed_xT = pack_weight(n((K, T)) * s)
    packed_w1 = pack_weight(n((K, H)) / np.sqrt(K) / s)
    packed_w2 = pack_weight(n((H, N)) / np.sqrt(2 * H) / u[:, None])
    packed_w3 = pack_weight(n((K, N)) / np.sqrt(2 * K) / s)
    return {
        "x_words": packed_xT[0],
        "x_scales": packed_xT[1],
        "w1_words": packed_w1[0],
        "w1_scales": packed_w1[1],
        "gn": (np.random.uniform(0.5, 1.5, (H, 1)) * u[:, None]).astype(np.float32),
        "w2_words": packed_w2[0],
        "w2_scales": packed_w2[1],
        "w3_words": packed_w3[0],
        "w3_scales": packed_w3[1],
        "offs": striped8(np.random.randint(0, T, (8, S))),
        "n1": striped(np.random.randint(0, S, W)),
        "two": striped(np.random.permutation(T)[:S]),
        "n2": striped(np.random.permutation(S)),
        "n3": striped(np.random.permutation(S)),
    }


def reference(x_words, x_scales, w1_words, w1_scales, gn, w2_words, w2_scales, w3_words, w3_scales, offs, n1, two, n2, n3):
    xq = unpack_weight(x_words, x_scales)[np.arange(K)[:, None], runs(offs, K)]
    y = unpack_weight(w1_words, w1_scales).T @ xq
    mb = y[:, unstriped(n1)]
    sq = (mb) ** 2
    qs = sq.reshape(H, S, 4).sum(axis=2)
    z = f64(gn) * (y / np.sqrt(qs + 0.5))
    x_two = unpack_weight(x_words, x_scales)[:, unstriped(two)]
    h = unpack_weight(w2_words, w2_scales).T @ mxq(z, 0, "e4m3") + unpack_weight(w3_words, w3_scales).T @ x_two
    out_0 = h[:, unstriped(n2)] / (np.abs(h) + np.abs(h[:, unstriped(n3)]) + 0.5)
    return (out_0,) + planes(out_0)

@@ -1,0 +1,254 @@
+from contextlib import ExitStack
+
+import concourse.mybir as mybir
+
+F32 = mybir.dt.float32
+BF16 = mybir.dt.bfloat16
+I32 = mybir.dt.int32
+U32 = mybir.dt.uint32
+U16 = mybir.dt.uint16
+U8 = mybir.dt.uint8
+FP8X4 = mybir.dt.float8_e4m3fn_x4
+ALU = mybir.AluOpType
+ACT = mybir.ActivationFunctionType
+AX = mybir.AxisListType
+
+P = 128
+PACK = 4
+T = 2048
+S = 512
+MEMBERS = 4
+LIST_ROWS = 16
+SPARE = 16
+SQUARES_ON_SCALAR = 2
+PLAIN_CHUNKS = 2
+SCALAR_ROUNDS = ()
+FLOPS = 3 * 2 * 512 * 512 * 512
+
+Z_CHUNKS = ((0, 256), (256, 128), (384, 128))
+Z_GROUPS = (((0, 256), 128), ((256, 128), 128), ((384, 64), 64), ((448, 64), 64))
+OUT_CHUNKS = ((0, 128), (128, 128), (256, 128), (384, 64), (448, 64))
+
+
+def words_view(dram):
+    return dram[0].rearrange("p n t -> p (n t)").bitcast(I32)
+
+
+def load_scale_rows(queue, tile, dram, first):
+    rows = dram[0].bitcast(I32)
+    for r in range(4):
+        queue.dma_start(out=tile[:].bitcast(I32)[first + r : P : 32, :], in_=rows[r:16:4, :])
+
+
+def deal(engine, dealt, raw):
+    engine.tensor_copy(out=dealt.rearrange("p (t m) -> p t m", t=PACK), in_=raw.rearrange("p (m t) -> p t m", t=PACK))
+
+
+def interleave(engine, woven, planes):
+    engine.tensor_copy(
+        out=woven.rearrange("p (c i t) -> p c t i", i=4, t=PACK),
+        in_=planes.rearrange("p t (c i) -> p c t i", i=4),
+    )
+
+
+def tile_picked_hmixgvarnorm2_none_po_kernel(
+    tc, x_words, x_scales, w1_words, w1_scales, gn, w2_words, w2_scales, w3_words, w3_scales,
+    offs, n1, two, n2, n3, out_0, out_1, out_2,
+):
+    nc = tc.nc
+    with ExitStack() as ctx:
+        keep = ctx.enter_context(tc.tile_pool(name="keep", bufs=1))
+        ring = ctx.enter_context(tc.tile_pool(name="ring", bufs=3))
+        outs = ctx.enter_context(tc.tile_pool(name="outs", bufs=2))
+        psum = ctx.enter_context(tc.psum_pool(name="psum", bufs=1))
+
+        def load_list(dram, name):
+            tile = keep.tile(list(dram.shape), U16, name=name)
+            nc.sync.dma_start(tile[:], dram)
+            return tile
+
+        xs = keep.tile([P, T], U8, name="xs", align_bytes=64)
+        w_sc_raw = keep.tile([P, S], U8, name="w_sc_raw", align_bytes=64)
+        xq_sc = keep.tile([P, S], U8, name="xq_sc", align_bytes=64)
+        x2_sc = keep.tile([P, S], U8, name="x2_sc", align_bytes=64)
+        nc.vector.memset(w_sc_raw[:].bitcast(I32), 0)
+        nc.vector.memset(xq_sc[:].bitcast(I32), 0)
+        nc.vector.memset(x2_sc[:].bitcast(I32), 0)
+        ysq = [keep.tile([P, S + SPARE], F32, name="ysq%d" % t) for t in range(PACK)]
+        for t in range(PACK):
+            nc.vector.memset(ysq[t][:, S:], 0.0)
+
+        offs_t = load_list(offs, "offs_t")
+        nc.sync.dma_start(out=xs[:].bitcast(I32), in_=x_scales[0].bitcast(I32).unsqueeze(1).broadcast_to([16, 8, T // 4]))
+        xw = keep.tile([P, T], U32, name="xw")
+        w_raw = keep.tile([P, S], I32, name="w_raw")
+        nc.sync.dma_start(out=xw[:].bitcast(I32), in_=words_view(x_words))
+        nc.sync.dma_start(out=w_raw[:], in_=words_view(w1_words))
+        load_scale_rows(nc.scalar, w_sc_raw, w1_scales, 0)
+        n1_t = load_list(n1, "n1_t")
+        two_t = load_list(two, "two_t")
+        gain = keep.tile([P, PACK], F32, name="gain")
+        nc.sync.dma_start(out=gain[:], in_=gn.rearrange("(p t) o -> p (t o)", t=PACK))
+
+        def pick_scales(offsets, plane, name, queues):
+            picked = keep.tile([P, S], U8, name=name, align_bytes=64)
+            nc.vector.tensor_copy(picked[:], xs[:].indirect(offsets[:]))
+            for r in range(4):
+                queues[r % len(queues)].dma_start(out=plane[:].bitcast(I32)[r:P:32, :], in_=picked[:].bitcast(I32)[8 * r : P : 32, :])
+
+        pick_scales(offs_t, xq_sc, "xq_sc_picked", (nc.scalar,))
+        w1_sc = keep.tile([P, S], U8, name="w1_sc", align_bytes=64)
+        deal(nc.vector, w1_sc[:], w_sc_raw[:])
+        w1 = keep.tile([P, S], I32, name="w1", align_bytes=64)
+        xq = keep.tile([P, S], U32, name="xq", align_bytes=64)
+        nc.vector.tensor_copy(xq[:], xw[:].indirect(offs_t[:]))
+        nc.vector.tensor_copy(w1[:, :P], w_raw[:, 0:S:PACK])
+        nc.vector.tensor_copy(w1[:, P:].rearrange("p (t m) -> p t m", t=PACK - 1), w_raw[:].rearrange("p (m t) -> p t m", t=PACK)[:, 1:, :])
+
+        y_ps = [psum.tile([P, S], F32, name="y_ps%d" % t, tag="bank%d" % t) for t in range(PACK)]
+        for t in range(PACK):
+            cols = slice(t * P, (t + 1) * P)
+            nc.tensor.matmul_mx(y_ps[t][:], lhsT=w1[:, cols].bitcast(FP8X4), lhsT_scale=w1_sc[:, cols],
+                                rhs=xq[:].bitcast(FP8X4), rhs_scale=xq_sc[:], start=True, stop=True)
+
+        for t in range(PACK):
+            if t < SQUARES_ON_SCALAR:
+                nc.scalar.activation(ysq[t][:, :S], y_ps[t][:], ACT.Square)
+            else:
+                y_copy = outs.tile([P, S], F32, name="y_copy")
+                nc.vector.tensor_copy(y_copy[:], y_ps[t][:])
+                nc.vector.tensor_tensor(ysq[t][:, :S], y_ps[t][:], y_copy[:], ALU.mult)
+
+        n3_t = load_list(n3, "n3_t")
+        n2_t = load_list(n2, "n2_t")
+        w2 = keep.tile([P, S], I32, name="w2", align_bytes=64)
+        w3 = keep.tile([P, S], I32, name="w3", align_bytes=64)
+        w23_sc = keep.tile([P, S], U8, name="w23_sc", align_bytes=64)
+        nc.sync.dma_start(out=w_raw[:], in_=words_view(w3_words))
+        load_scale_rows(nc.sync, w_sc_raw, w2_scales, 0)
+        load_scale_rows(nc.sync, w_sc_raw, w3_scales, 4)
+        x2 = keep.tile([P, S], U32, name="x2", align_bytes=64)
+        nc.vector.tensor_copy(x2[:], xw[:].indirect(two_t[:]))
+        pick_scales(two_t, x2_sc, "x2_sc_picked", (nc.sync,))
+        deal(nc.vector, w3[:], w_raw[:])
+        nc.sync.dma_start(out=w_raw[:], in_=words_view(w2_words))
+        deal(nc.vector, w23_sc[:], w_sc_raw[:])
+        deal(nc.vector, w2[:], w_raw[:])
+
+        qs = keep.tile([P, PACK, S], F32, name="qs")
+        rs = keep.tile([P, PACK, S], F32, name="rs")
+        zb = keep.tile([P, PACK, S], BF16, name="zb")
+        zi = keep.tile([P, S * PACK], BF16, name="zi", align_bytes=64)
+        zq = keep.tile([P, S], U32, name="zq", align_bytes=64)
+        z_sc = keep.tile([P, S], U8, name="z_sc", align_bytes=64)
+        h = [keep.tile([P, S], F32, name="h%d" % t) for t in range(PACK)]
+        habs = keep.tile([P, PACK * S], F32, name="habs")
+        last0, last_w = Z_CHUNKS[-1]
+        h_ps = [[psum.tile([P, 2, w], F32, name="h_ps%d_%d" % (c, u), tag="bank%d" % (PACK + 2 * (c % 2) + u)) for u in range(2)]
+                for c, (c0, w) in enumerate(Z_CHUNKS)]
+
+        def pass_w3(bank, t, c0, w, start):
+            cols = slice(t * P, (t + 1) * P)
+            nc.tensor.matmul_mx(bank, lhsT=w3[:, cols].bitcast(FP8X4), lhsT_scale=w23_sc[4:P, cols],
+                                rhs=x2[:, c0 : c0 + w].bitcast(FP8X4), rhs_scale=x2_sc[:, c0 : c0 + w], start=start, stop=False)
+
+        def pass_w2(bank, t, c0, w, stop):
+            cols = slice(t * P, (t + 1) * P)
+            nc.tensor.matmul_mx(bank, lhsT=w2[:, cols].bitcast(FP8X4), lhsT_scale=w23_sc[:, cols],
+                                rhs=zq[:, c0 : c0 + w].bitcast(FP8X4), rhs_scale=z_sc[:, c0 : c0 + w], start=False, stop=stop)
+
+        def open_h(c):
+            c0, w = Z_CHUNKS[c]
+            for t in range(PACK):
+                pass_w3(h_ps[c][t // 2][:, t % 2, :], t, c0, w, t % 2 == 0)
+
+        def gathers(group):
+            (g0, gw), piece = group
+            for t in range(PACK):
+                for c0 in range(g0, g0 + gw, piece):
+                    n = piece * MEMBERS
+                    members = ring.tile([P, 128 * MEMBERS], F32, name="members")
+                    o0 = c0 * MEMBERS // LIST_ROWS
+                    nc.scalar.activation(members[:, :n], ysq[t][:].indirect(n1_t[:, o0 : o0 + n // LIST_ROWS]), ACT.Copy)
+                    nc.vector.tensor_reduce(qs[:, t, c0 : c0 + piece], members[:, :n].rearrange("p (j m) -> p j m", m=MEMBERS),
+                                            axis=AX.X, op=ALU.add)
+
+        def make_z(group):
+            (g0, gw), piece = group
+            cols = slice(g0, g0 + gw)
+            nc.scalar.activation(rs[:, :, cols], qs[:, :, cols], ACT.Abs_reciprocal_sqrt, bias=0.5)
+            for t in range(PACK):
+                nc.vector.scalar_tensor_tensor(zb[:, t, cols], y_ps[t][:, cols], gain[:, t : t + 1], rs[:, t, cols], ALU.mult, ALU.mult)
+            woven = zi[:, g0 * PACK : (g0 + gw) * PACK]
+            interleave(nc.vector, woven, zb[:, :, cols])
+            nc.vector.quantize_mx(zq[:, cols].bitcast(FP8X4), z_sc[:, cols], woven)
+
+        habs3 = habs[:].rearrange("p (t j) -> p t j", t=PACK)
+
+        def close_h(c):
+            c0, w = Z_CHUNKS[c]
+            cols = slice(c0, c0 + w)
+            for t in range(PACK):
+                pass_w2(h_ps[c][t // 2][:, t % 2, :], t, c0, w, t % 2 == 1)
+            if c0 == last0:
+                nc.scalar.activation(habs3[:, 0:2, cols], h_ps[c][0][:], ACT.Abs)
+                for t in (2, 3):
+                    nc.vector.tensor_copy(h[t][:, cols], h_ps[c][1][:, t % 2, :])
+                nc.scalar.activation(habs3[:, 2:4, cols], h_ps[c][1][:], ACT.Abs)
+                for t in (0, 1):
+                    nc.vector.tensor_copy(h[t][:, cols], h_ps[c][0][:, t % 2, :])
+            else:
+                for t in range(PACK):
+                    nc.vector.tensor_copy(h[t][:, cols], h_ps[c][t // 2][:, t % 2, :])
+                for t in range(PACK):
+                    nc.vector.scalar_tensor_tensor(habs3[:, t, cols], h_ps[c][t // 2][:, t % 2, :], -1.0, h[t][:, cols], ALU.mult, ALU.max)
+
+        ends = dict((c0 + w, c) for c, (c0, w) in enumerate(Z_CHUNKS))
+        open_h(0)
+        open_h(1)
+        for group in Z_GROUPS:
+            gathers(group)
+            make_z(group)
+            end = group[0][0] + group[0][1]
+            if end in ends:
+                close_h(ends[end])
+                if ends[end] + 2 < len(Z_CHUNKS):
+                    open_h(ends[end] + 2)
+
+        o_words = keep.tile([P, S], U32, name="o_words", align_bytes=64)
+        o_sc = keep.tile([P, S], U8, name="o_sc", align_bytes=64)
+        out_rows = out_0.rearrange("(p t) j -> p t j", t=PACK)
+        out_words = words_view(out_1)
+        for c, (c0, w) in enumerate(OUT_CHUNKS):
+            cols = slice(c0, c0 + w)
+            lcols = slice(c0 // LIST_ROWS, (c0 + w) // LIST_ROWS)
+            other = outs.tile([P, PACK, w], F32, name="other%d" % w)
+            for t in range(PACK):
+                nc.scalar.activation(other[:, t, :], habs[:, t * S : (t + 1) * S].indirect(n3_t[:, lcols]), ACT.Copy)
+            if c < PLAIN_CHUNKS:
+                top = outs.tile([P, PACK, w], F32, name="top%d" % w)
+                for t in range(PACK):
+                    nc.vector.tensor_copy(top[:, t, :], h[t][:].indirect(n2_t[:, lcols]))
+            den = outs.tile([P, PACK, w], F32, name="den%d" % w)
+            nc.vector.tensor_tensor(den[:], habs3[:, :, cols], other[:], ALU.add)
+            root = outs.tile([P, PACK, w], F32, name="root%d" % w)
+            nc.scalar.activation(root[:], den[:], ACT.Abs_reciprocal_sqrt, bias=0.5)
+            rec = outs.tile([P, PACK, w], F32, name="rec%d" % w)
+            nc.scalar.activation(rec[:], root[:], ACT.Square)
+            res = outs.tile([P, PACK, w], F32, name="res%d" % w, bufs=4)
+            if c < PLAIN_CHUNKS:
+                nc.vector.tensor_tensor(res[:], top[:], rec[:], ALU.mult)
+            else:
+                for t in range(PACK):
+                    nc.vector.tensor_tensor(res[:, t, :], h[t][:].indirect(n2_t[:, lcols]), rec[:, t, :], ALU.mult)
+            nc.sync.dma_start(out=out_rows[:, :, cols], in_=res[:])
+            woven = outs.tile([P, PACK * w], BF16, name="woven%d" % w, align_bytes=64)
+            if c in SCALAR_ROUNDS:
+                nc.scalar.copy(woven[:].rearrange("p (c i t) -> p c t i", i=4, t=PACK), res[:].rearrange("p t (c i) -> p c t i", i=4))
+            else:
+                interleave(nc.vector, woven[:], res[:])
+            nc.vector.quantize_mx(o_words[:, cols].bitcast(FP8X4), o_sc[:, cols], woven[:])
+            nc.sync.dma_start(out=out_words[:, cols], in_=o_words[:, cols].bitcast(I32))
+        sc_rows = out_2[0].bitcast(I32)
+        for r in range(4):
+            (nc.scalar if r % 2 else nc.sync).dma_start(out=sc_rows[r:16:4, :], in_=o_sc[:].bitcast(I32)[r:P:32, :])

@@ -1,6 +1,7 @@
 from contextlib import ExitStack
 
 import concourse.mybir as mybir
+from concourse.masks import make_identity
 
 F32 = mybir.dt.float32
 BF16 = mybir.dt.bfloat16
@@ -11,44 +12,40 @@ U8 = mybir.dt.uint8
 FP8X4 = mybir.dt.float8_e4m3fn_x4
 ALU = mybir.AluOpType
 ACT = mybir.ActivationFunctionType
-AX = mybir.AxisListType
 
 P = 128
-PACK = 4
+PLANES = 4
+BLOCKS = 16
 T = 2048
 S = 512
 MEMBERS = 4
 LIST_ROWS = 16
 SPARE = 16
-SQUARES_ON_SCALAR = 2
-PLAIN_CHUNKS = 2
-SCALAR_ROUNDS = ()
+CHUNK = 128
+HALF = 0.5
 FLOPS = 3 * 2 * 512 * 512 * 512
 
-Z_CHUNKS = ((0, 256), (256, 128), (384, 128))
-Z_GROUPS = (((0, 256), 128), ((256, 128), 128), ((384, 64), 64), ((448, 64), 64))
-OUT_CHUNKS = ((0, 128), (128, 128), (256, 128), (384, 64), (448, 64))
+GROUPS = ((0, 128), (128, 128), (256, 128), (384, 64), (448, 64))
+GATHERS = ((0, 0), (1, 0), (0, 1), (0, 2), (0, 3), (1, 1), (1, 2), (1, 3)) + tuple((g, t) for g in (2, 3, 4) for t in range(PLANES))
 
 
 def words_view(dram):
     return dram[0].rearrange("p n t -> p (n t)").bitcast(I32)
 
 
-def load_scale_rows(queue, tile, dram, first):
-    rows = dram[0].bitcast(I32)
-    for r in range(4):
-        queue.dma_start(out=tile[:].bitcast(I32)[first + r : P : 32, :], in_=rows[r:16:4, :])
-
-
 def deal(engine, dealt, raw):
-    engine.tensor_copy(out=dealt.rearrange("p (t m) -> p t m", t=PACK), in_=raw.rearrange("p (m t) -> p t m", t=PACK))
+    engine.tensor_copy(out=dealt.rearrange("p (t m) -> p t m", t=PLANES), in_=raw.rearrange("p (m t) -> p t m", t=PLANES))
 
 
-def interleave(engine, woven, planes):
-    engine.tensor_copy(
-        out=woven.rearrange("p (c i t) -> p c t i", i=4, t=PACK),
+def weave(nc, woven, planes):
+    nc.vector.tensor_copy(
+        out=woven.rearrange("p (c i t) -> p c t i", i=4, t=PLANES),
         in_=planes.rearrange("p t (c i) -> p c t i", i=4),
     )
+
+
+def entries(first, count):
+    return slice(first // LIST_ROWS, (first + count) // LIST_ROWS)
 
 
 def tile_picked_hmixgvarnorm2_none_po_kernel(
@@ -59,7 +56,6 @@ def tile_picked_hmixgvarnorm2_none_po_kernel(
     with ExitStack() as ctx:
         keep = ctx.enter_context(tc.tile_pool(name="keep", bufs=1))
         ring = ctx.enter_context(tc.tile_pool(name="ring", bufs=3))
-        outs = ctx.enter_context(tc.tile_pool(name="outs", bufs=2))
         psum = ctx.enter_context(tc.psum_pool(name="psum", bufs=1))
 
         def load_list(dram, name):
@@ -67,188 +63,233 @@ def tile_picked_hmixgvarnorm2_none_po_kernel(
             nc.sync.dma_start(tile[:], dram)
             return tile
 
-        xs = keep.tile([P, T], U8, name="xs", align_bytes=64)
-        w_sc_raw = keep.tile([P, S], U8, name="w_sc_raw", align_bytes=64)
+        def bank(b, shape, name):
+            return psum.tile(shape, F32, name=name, tag="bank%d" % b)
+
         xq_sc = keep.tile([P, S], U8, name="xq_sc", align_bytes=64)
         x2_sc = keep.tile([P, S], U8, name="x2_sc", align_bytes=64)
-        nc.vector.memset(w_sc_raw[:].bitcast(I32), 0)
         nc.vector.memset(xq_sc[:].bitcast(I32), 0)
         nc.vector.memset(x2_sc[:].bitcast(I32), 0)
-        ysq = [keep.tile([P, S + SPARE], F32, name="ysq%d" % t) for t in range(PACK)]
-        for t in range(PACK):
+        ysq = [keep.tile([P, S + SPARE], F32, name="ysq%d" % t) for t in range(PLANES)]
+        for t in range(PLANES):
             nc.vector.memset(ysq[t][:, S:], 0.0)
+        warm_in = keep.tile([P, 1], F32, name="warm_in")
+        warm_out = keep.tile([P, 1], F32, name="warm_out")
+        nc.vector.memset(warm_in[:], 1.0)
+        nc.scalar.activation(warm_out[:], warm_in[:], ACT.Abs_reciprocal_sqrt)
+        ident = keep.tile([P, P], F32, name="ident")
+        make_identity(nc, ident[:])
 
+        xs = keep.tile([P, T], U8, name="xs")
+        nc.sync.dma_start(out=xs[:].bitcast(I32), in_=x_scales[0].bitcast(I32).unsqueeze(1).broadcast_to([BLOCKS, P // BLOCKS, T // 4]))
         offs_t = load_list(offs, "offs_t")
-        nc.sync.dma_start(out=xs[:].bitcast(I32), in_=x_scales[0].bitcast(I32).unsqueeze(1).broadcast_to([16, 8, T // 4]))
         xw = keep.tile([P, T], U32, name="xw")
-        w_raw = keep.tile([P, S], I32, name="w_raw")
         nc.sync.dma_start(out=xw[:].bitcast(I32), in_=words_view(x_words))
+        w_raw = keep.tile([P, S], I32, name="w_raw")
         nc.sync.dma_start(out=w_raw[:], in_=words_view(w1_words))
-        load_scale_rows(nc.scalar, w_sc_raw, w1_scales, 0)
+        w_sc_raw = keep.tile([P, S], U8, name="w_sc_raw")
+        for q in range(4):
+            rows = w1_scales[0].bitcast(I32)[4 * q : 4 * q + 4, :]
+            nc.scalar.dma_start(out=w_sc_raw[:].bitcast(I32)[32 * q : 32 * q + 32, :], in_=rows.unsqueeze(0).broadcast_to([8, 4, S // 4]))
         n1_t = load_list(n1, "n1_t")
         two_t = load_list(two, "two_t")
-        gain = keep.tile([P, PACK], F32, name="gain")
-        nc.sync.dma_start(out=gain[:], in_=gn.rearrange("(p t) o -> p (t o)", t=PACK))
+        gain = keep.tile([P, PLANES], F32, name="gain")
+        nc.gpsimd.dma_start(out=gain[:], in_=gn.rearrange("(p t) o -> p (t o)", t=PLANES))
 
-        def pick_scales(offsets, plane, name, queues):
-            picked = keep.tile([P, S], U8, name=name, align_bytes=64)
+        def pick_scales(offsets, plane, name, tag, queues):
+            picked = keep.tile([P, S], U8, name=name, tag=tag, align_bytes=64)
             nc.vector.tensor_copy(picked[:], xs[:].indirect(offsets[:]))
             for r in range(4):
                 queues[r % len(queues)].dma_start(out=plane[:].bitcast(I32)[r:P:32, :], in_=picked[:].bitcast(I32)[8 * r : P : 32, :])
 
-        pick_scales(offs_t, xq_sc, "xq_sc_picked", (nc.scalar,))
+        pick_scales(offs_t, xq_sc, "xq_picked", "xq_picked", (nc.scalar, nc.sync))
         w1_sc = keep.tile([P, S], U8, name="w1_sc", align_bytes=64)
         deal(nc.vector, w1_sc[:], w_sc_raw[:])
-        w1 = keep.tile([P, S], I32, name="w1", align_bytes=64)
         xq = keep.tile([P, S], U32, name="xq", align_bytes=64)
         nc.vector.tensor_copy(xq[:], xw[:].indirect(offs_t[:]))
-        nc.vector.tensor_copy(w1[:, :P], w_raw[:, 0:S:PACK])
-        nc.vector.tensor_copy(w1[:, P:].rearrange("p (t m) -> p t m", t=PACK - 1), w_raw[:].rearrange("p (m t) -> p t m", t=PACK)[:, 1:, :])
+        w1 = keep.tile([P, S], I32, name="w1", align_bytes=64)
+        deal(nc.vector, w1[:], w_raw[:])
 
-        y_ps = [psum.tile([P, S], F32, name="y_ps%d" % t, tag="bank%d" % t) for t in range(PACK)]
-        for t in range(PACK):
+        y_ps = [bank(t, [P, S], "y_ps%d" % t) for t in range(PLANES)]
+        for t in range(PLANES):
             cols = slice(t * P, (t + 1) * P)
             nc.tensor.matmul_mx(y_ps[t][:], lhsT=w1[:, cols].bitcast(FP8X4), lhsT_scale=w1_sc[:, cols],
                                 rhs=xq[:].bitcast(FP8X4), rhs_scale=xq_sc[:], start=True, stop=True)
-
-        for t in range(PACK):
-            if t < SQUARES_ON_SCALAR:
-                nc.scalar.activation(ysq[t][:, :S], y_ps[t][:], ACT.Square)
-            else:
-                y_copy = outs.tile([P, S], F32, name="y_copy")
-                nc.vector.tensor_copy(y_copy[:], y_ps[t][:])
-                nc.vector.tensor_tensor(ysq[t][:, :S], y_ps[t][:], y_copy[:], ALU.mult)
+        nc.scalar.activation(ysq[0][:, :S], y_ps[0][:], ACT.Square)
+        for t in range(1, PLANES):
+            y_copy = keep.tile([P, S], F32, name="y_copy%d" % t, tag="y_copy%d" % t, align_bytes=64)
+            nc.vector.tensor_copy(y_copy[:], y_ps[t][:])
+            nc.vector.tensor_tensor(ysq[t][:, :S], y_ps[t][:], y_copy[:], ALU.mult)
 
         n3_t = load_list(n3, "n3_t")
         n2_t = load_list(n2, "n2_t")
         w2 = keep.tile([P, S], I32, name="w2", align_bytes=64)
-        w3 = keep.tile([P, S], I32, name="w3", align_bytes=64)
+        w3 = keep.tile([P, S], I32, name="w3", tag="y_copy2", align_bytes=64)
         w23_sc = keep.tile([P, S], U8, name="w23_sc", align_bytes=64)
         nc.sync.dma_start(out=w_raw[:], in_=words_view(w3_words))
-        load_scale_rows(nc.sync, w_sc_raw, w2_scales, 0)
-        load_scale_rows(nc.sync, w_sc_raw, w3_scales, 4)
+        for first, scales in ((0, w2_scales), (4, w3_scales)):
+            for r in range(4):
+                nc.sync.dma_start(out=w_sc_raw[:].bitcast(I32)[first + r : P : 32, :], in_=scales[0].bitcast(I32)[r:BLOCKS:4, :])
         x2 = keep.tile([P, S], U32, name="x2", align_bytes=64)
         nc.vector.tensor_copy(x2[:], xw[:].indirect(two_t[:]))
-        pick_scales(two_t, x2_sc, "x2_sc_picked", (nc.sync,))
+        pick_scales(two_t, x2_sc, "x2_picked", "y_copy3", (nc.sync,))
         deal(nc.vector, w3[:], w_raw[:])
         nc.sync.dma_start(out=w_raw[:], in_=words_view(w2_words))
         deal(nc.vector, w23_sc[:], w_sc_raw[:])
         deal(nc.vector, w2[:], w_raw[:])
 
-        qs = keep.tile([P, PACK, S], F32, name="qs")
-        rs = keep.tile([P, PACK, S], F32, name="rs")
-        zb = keep.tile([P, PACK, S], BF16, name="zb")
-        zi = keep.tile([P, S * PACK], BF16, name="zi", align_bytes=64)
+        qs = keep.tile([P, PLANES, S], F32, name="qs")
+        rs = keep.tile([P, PLANES, S], F32, name="rs")
+        zb = keep.tile([P, PLANES, S], BF16, name="zb")
+        z_woven = keep.tile([P, S * PLANES], BF16, name="z_woven", align_bytes=64)
         zq = keep.tile([P, S], U32, name="zq", align_bytes=64)
         z_sc = keep.tile([P, S], U8, name="z_sc", align_bytes=64)
-        h = [keep.tile([P, S], F32, name="h%d" % t) for t in range(PACK)]
-        habs = keep.tile([P, PACK * S], F32, name="habs")
-        last0, last_w = Z_CHUNKS[-1]
-        h_ps = [[psum.tile([P, 2, w], F32, name="h_ps%d_%d" % (c, u), tag="bank%d" % (PACK + 2 * (c % 2) + u)) for u in range(2)]
-                for c, (c0, w) in enumerate(Z_CHUNKS)]
+        h_both = keep.tile([P, 2 * PLANES * S], F32, name="h_both")
+        h = h_both[:, : PLANES * S].rearrange("p (t j) -> p t j", t=PLANES)
+        h_abs = h_both[:, PLANES * S :].rearrange("p (t j) -> p t j", t=PLANES)
+        chunks = S // CHUNK
+        h_ps = [[bank(PLANES + 2 * (c % 2) + u, [P, 2, CHUNK], "h_ps%d_%d" % (c, u)) for u in range(2)] for c in range(chunks)]
+        last_group = len(GROUPS) - 1
+        last_cols = slice(S - CHUNK, S)
 
-        def pass_w3(bank, t, c0, w, start):
-            cols = slice(t * P, (t + 1) * P)
-            nc.tensor.matmul_mx(bank, lhsT=w3[:, cols].bitcast(FP8X4), lhsT_scale=w23_sc[4:P, cols],
-                                rhs=x2[:, c0 : c0 + w].bitcast(FP8X4), rhs_scale=x2_sc[:, c0 : c0 + w], start=start, stop=False)
+        def sums(g):
+            first, width = GROUPS[g]
+            return h_abs[:, :, :width] if g == last_group else qs[:, :, first : first + width]
 
-        def pass_w2(bank, t, c0, w, stop):
-            cols = slice(t * P, (t + 1) * P)
-            nc.tensor.matmul_mx(bank, lhsT=w2[:, cols].bitcast(FP8X4), lhsT_scale=w23_sc[:, cols],
-                                rhs=zq[:, c0 : c0 + w].bitcast(FP8X4), rhs_scale=z_sc[:, c0 : c0 + w], start=False, stop=stop)
+        def h_pass(c, weights, plane_row, codes, scales, opens):
+            cols = slice(c * CHUNK, (c + 1) * CHUNK)
+            for t in range(PLANES):
+                w_cols = slice(t * P, (t + 1) * P)
+                nc.tensor.matmul_mx(h_ps[c][t // 2][:, t % 2, :], lhsT=weights[:, w_cols].bitcast(FP8X4), lhsT_scale=w23_sc[plane_row:P, w_cols],
+                                    rhs=codes[:, cols].bitcast(FP8X4), rhs_scale=scales[:, cols],
+                                    start=opens and t % 2 == 0, stop=not opens and t % 2 == 1)
 
-        def open_h(c):
-            c0, w = Z_CHUNKS[c]
-            for t in range(PACK):
-                pass_w3(h_ps[c][t // 2][:, t % 2, :], t, c0, w, t % 2 == 0)
+        def gather_members(g, t):
+            first, width = GROUPS[g]
+            n = width * MEMBERS
+            members = ring.tile([P, CHUNK * MEMBERS], F32, name="members")
+            nc.scalar.activation(members[:, :n], ysq[t][:].indirect(n1_t[:, entries(first * MEMBERS, n)]), ACT.Copy)
+            nc.vector.tensor_reduce(sums(g)[:, t, :], members[:, :n].rearrange("p (j m) -> p j m", m=MEMBERS),
+                                    axis=mybir.AxisListType.X, op=ALU.add)
 
-        def gathers(group):
-            (g0, gw), piece = group
-            for t in range(PACK):
-                for c0 in range(g0, g0 + gw, piece):
-                    n = piece * MEMBERS
-                    members = ring.tile([P, 128 * MEMBERS], F32, name="members")
-                    o0 = c0 * MEMBERS // LIST_ROWS
-                    nc.scalar.activation(members[:, :n], ysq[t][:].indirect(n1_t[:, o0 : o0 + n // LIST_ROWS]), ACT.Copy)
-                    nc.vector.tensor_reduce(qs[:, t, c0 : c0 + piece], members[:, :n].rearrange("p (j m) -> p j m", m=MEMBERS),
-                                            axis=AX.X, op=ALU.add)
+        def scale_z(g):
+            first, width = GROUPS[g]
+            cols = slice(first, first + width)
+            for t0, t1 in ((0, PLANES - 1), (PLANES - 1, PLANES)) if g == last_group else ((0, PLANES),):
+                nc.scalar.activation(rs[:, t0:t1, cols], sums(g)[:, t0:t1, :], ACT.Abs_reciprocal_sqrt, bias=HALF)
+                for t in range(t0, t1):
+                    nc.vector.scalar_tensor_tensor(zb[:, t, cols], y_ps[t][:, cols], gain[:, t : t + 1], rs[:, t, cols], ALU.mult, ALU.mult)
 
-        def make_z(group):
-            (g0, gw), piece = group
-            cols = slice(g0, g0 + gw)
-            nc.scalar.activation(rs[:, :, cols], qs[:, :, cols], ACT.Abs_reciprocal_sqrt, bias=0.5)
-            for t in range(PACK):
-                nc.vector.scalar_tensor_tensor(zb[:, t, cols], y_ps[t][:, cols], gain[:, t : t + 1], rs[:, t, cols], ALU.mult, ALU.mult)
-            woven = zi[:, g0 * PACK : (g0 + gw) * PACK]
-            interleave(nc.vector, woven, zb[:, :, cols])
+        def quantise_z(g):
+            first, width = GROUPS[g]
+            cols = slice(first, first + width)
+            woven = z_woven[:, first * PLANES : (first + width) * PLANES]
+            weave(nc, woven, zb[:, :, cols])
             nc.vector.quantize_mx(zq[:, cols].bitcast(FP8X4), z_sc[:, cols], woven)
+            if (first + width) % CHUNK == 0:
+                h_pass(first // CHUNK, w2, 0, zq, z_sc, False)
 
-        habs3 = habs[:].rearrange("p (t j) -> p t j", t=PACK)
+        def copy_h(c):
+            for u in range(2):
+                nc.vector.tensor_copy(h[:, 2 * u : 2 * u + 2, c * CHUNK : (c + 1) * CHUNK], h_ps[c][u][:])
+            if c + 2 < chunks:
+                h_pass(c + 2, w3, 4, x2, x2_sc, True)
 
-        def close_h(c):
-            c0, w = Z_CHUNKS[c]
-            cols = slice(c0, c0 + w)
-            for t in range(PACK):
-                pass_w2(h_ps[c][t // 2][:, t % 2, :], t, c0, w, t % 2 == 1)
-            if c0 == last0:
-                nc.scalar.activation(habs3[:, 0:2, cols], h_ps[c][0][:], ACT.Abs)
-                for t in (2, 3):
-                    nc.vector.tensor_copy(h[t][:, cols], h_ps[c][1][:, t % 2, :])
-                nc.scalar.activation(habs3[:, 2:4, cols], h_ps[c][1][:], ACT.Abs)
-                for t in (0, 1):
-                    nc.vector.tensor_copy(h[t][:, cols], h_ps[c][0][:, t % 2, :])
-            else:
-                for t in range(PACK):
-                    nc.vector.tensor_copy(h[t][:, cols], h_ps[c][t // 2][:, t % 2, :])
-                for t in range(PACK):
-                    nc.vector.scalar_tensor_tensor(habs3[:, t, cols], h_ps[c][t // 2][:, t % 2, :], -1.0, h[t][:, cols], ALU.mult, ALU.max)
-
-        ends = dict((c0 + w, c) for c, (c0, w) in enumerate(Z_CHUNKS))
-        open_h(0)
-        open_h(1)
-        for group in Z_GROUPS:
-            gathers(group)
-            make_z(group)
-            end = group[0][0] + group[0][1]
-            if end in ends:
-                close_h(ends[end])
-                if ends[end] + 2 < len(Z_CHUNKS):
-                    open_h(ends[end] + 2)
+        h_pass(0, w3, 4, x2, x2_sc, True)
+        h_pass(1, w3, 4, x2, x2_sc, True)
+        summed = None
+        age = 0
+        for g, t in GATHERS:
+            gather_members(g, t)
+            if summed is not None:
+                age = age + 1
+                if age == 1:
+                    scale_z(summed)
+                if age == 2:
+                    quantise_z(summed)
+                if age == 3 and summed < chunks - 1:
+                    copy_h(summed)
+            if t == PLANES - 1:
+                summed = g
+                age = 0
+        scale_z(last_group)
+        quantise_z(last_group)
+        nc.scalar.activation(h_abs[:, :, : S - CHUNK], h[:, :, : S - CHUNK], ACT.Abs)
+        for u in range(2):
+            nc.scalar.activation(h_abs[:, 2 * u : 2 * u + 2, last_cols], h_ps[-1][u][:], ACT.Abs)
+            nc.vector.tensor_copy(h[:, 2 - 2 * u : 4 - 2 * u, last_cols], h_ps[-1][1 - u][:])
 
         o_words = keep.tile([P, S], U32, name="o_words", align_bytes=64)
         o_sc = keep.tile([P, S], U8, name="o_sc", align_bytes=64)
-        out_rows = out_0.rearrange("(p t) j -> p t j", t=PACK)
+        out_rows = out_0.rearrange("(p t) j -> p t j", t=PLANES)
         out_words = words_view(out_1)
-        for c, (c0, w) in enumerate(OUT_CHUNKS):
-            cols = slice(c0, c0 + w)
-            lcols = slice(c0 // LIST_ROWS, (c0 + w) // LIST_ROWS)
-            other = outs.tile([P, PACK, w], F32, name="other%d" % w)
-            for t in range(PACK):
-                nc.scalar.activation(other[:, t, :], habs[:, t * S : (t + 1) * S].indirect(n3_t[:, lcols]), ACT.Copy)
-            if c < PLAIN_CHUNKS:
-                top = outs.tile([P, PACK, w], F32, name="top%d" % w)
-                for t in range(PACK):
-                    nc.vector.tensor_copy(top[:, t, :], h[t][:].indirect(n2_t[:, lcols]))
-            den = outs.tile([P, PACK, w], F32, name="den%d" % w)
-            nc.vector.tensor_tensor(den[:], habs3[:, :, cols], other[:], ALU.add)
-            root = outs.tile([P, PACK, w], F32, name="root%d" % w)
-            nc.scalar.activation(root[:], den[:], ACT.Abs_reciprocal_sqrt, bias=0.5)
-            rec = outs.tile([P, PACK, w], F32, name="rec%d" % w)
-            nc.scalar.activation(rec[:], root[:], ACT.Square)
-            res = outs.tile([P, PACK, w], F32, name="res%d" % w, bufs=4)
-            if c < PLAIN_CHUNKS:
-                nc.vector.tensor_tensor(res[:], top[:], rec[:], ALU.mult)
+        top = keep.tile([P, PLANES, S], F32, name="top")
+        for t in range(PLANES):
+            nc.vector.tensor_copy(top[:, t, :], h_both[:, t * S : (t + 2) * S].indirect(n2_t[:]))
+
+        def gather_other(other, planes, first, width):
+            for i, t in enumerate(planes):
+                nc.scalar.activation(other[:, i, :], h_abs[:, t, :].indirect(n3_t[:, entries(first, width)]), ACT.Copy)
+
+        def weave_out(res, name, on_gpsimd):
+            woven = keep.tile([P, PLANES * res.shape[2]], BF16, name=name, align_bytes=64)
+            if on_gpsimd:
+                nc.gpsimd.tensor_scalar(woven[:].rearrange("p (c i t) -> p c t i", i=4, t=PLANES), res[:].rearrange("p t (c i) -> p c t i", i=4),
+                                        1.0, 0.0, ALU.mult, ALU.add)
             else:
-                for t in range(PACK):
-                    nc.vector.tensor_tensor(res[:, t, :], h[t][:].indirect(n2_t[:, lcols]), rec[:, t, :], ALU.mult)
-            nc.sync.dma_start(out=out_rows[:, :, cols], in_=res[:])
-            woven = outs.tile([P, PACK * w], BF16, name="woven%d" % w, align_bytes=64)
-            if c in SCALAR_ROUNDS:
-                nc.scalar.copy(woven[:].rearrange("p (c i t) -> p c t i", i=4, t=PACK), res[:].rearrange("p t (c i) -> p c t i", i=4))
-            else:
-                interleave(nc.vector, woven[:], res[:])
+                weave(nc, woven[:], res[:])
+            return woven
+
+        def quantise_out(woven, cols):
             nc.vector.quantize_mx(o_words[:, cols].bitcast(FP8X4), o_sc[:, cols], woven[:])
             nc.sync.dma_start(out=out_words[:, cols], in_=o_words[:, cols].bitcast(I32))
-        sc_rows = out_2[0].bitcast(I32)
+
+        wide = S // 2
+        wide_cols = slice(0, wide)
+        turns = 2 * wide // P
+        root_wide = keep.tile([P, 2, 2 * wide], F32, name="root_wide", tag="root_wide")
+        res_wide = keep.tile([P, PLANES, wide], F32, name="res_wide")
+        den_ps = [bank(u, [P, turns, P], "den_ps%d" % u) for u in range(2)]
+        rec_ps = [bank(2 + u, [P, turns, P], "rec_ps%d" % u) for u in range(2)]
+        for u in range(2):
+            other = keep.tile([P, 2, wide], F32, name="other_wide%d" % u)
+            gather_other(other, (2 * u, 2 * u + 1), 0, wide)
+            for b in range(turns):
+                own = h_abs[:, 2 * u + b // 2, (b % 2) * P : (b % 2 + 1) * P]
+                nc.tensor.matmul(den_ps[u][:, b, :], lhsT=own, rhs=ident[:], is_transpose=True, start=b == 0, stop=False)
+            for b in range(turns):
+                nc.tensor.matmul(den_ps[u][:, b, :], lhsT=other[:, b // 2, (b % 2) * P : (b % 2 + 1) * P], rhs=ident[:],
+                                 is_transpose=True, start=False, stop=b == turns - 1)
+        rec_wide = [keep.tile([P, turns * P], F32, name="rec_wide%d" % u, tag="rec_wide%d" % u) for u in range(2)]
+        for u in range(2):
+            nc.scalar.activation(root_wide[:, u, :], den_ps[u][:].rearrange("p b j -> p (b j)"), ACT.Abs_reciprocal_sqrt, bias=HALF)
+            nc.scalar.activation(rec_wide[u][:], root_wide[:, u, :], ACT.Square)
+            for b in range(turns):
+                nc.tensor.transpose(rec_ps[u][:, b, :], rec_wide[u][:, b * P : (b + 1) * P], ident[:])
+        for u in range(2):
+            planes = slice(2 * u, 2 * u + 2)
+            nc.vector.tensor_tensor(res_wide[:, planes, :], top[:, planes, wide_cols],
+                                    rec_ps[u][:].rearrange("p (t c) j -> p t (c j)", t=2), ALU.mult)
+            nc.sync.dma_start(out=out_rows[:, planes, wide_cols], in_=res_wide[:, planes, :])
+
+        narrow = [slice(wide + v * CHUNK, wide + (v + 1) * CHUNK) for v in range(2)]
+        other_narrow = keep.tile([P, 2, PLANES, CHUNK], F32, name="other_narrow", tag="root_wide")
+        den = [keep.tile([P, PLANES, CHUNK], F32, name="den%d" % v, tag="rec_wide%d" % (1 - v)) for v in range(2)]
+        for v in range(2):
+            gather_other(other_narrow[:, v], range(PLANES), narrow[v].start, CHUNK)
+        nc.vector.tensor_tensor(den[0][:], h_abs[:, :, narrow[0]], other_narrow[:, 0], ALU.add)
+        woven_wide = weave_out(res_wide, "woven_wide", False)
+        nc.vector.tensor_tensor(den[1][:], h_abs[:, :, narrow[1]], other_narrow[:, 1], ALU.add)
+        quantise_out(woven_wide, wide_cols)
+        for v in range(2):
+            root = keep.tile([P, PLANES, CHUNK], F32, name="root%d" % v)
+            rec = keep.tile([P, PLANES, CHUNK], F32, name="rec%d" % v)
+            res = keep.tile([P, PLANES, CHUNK], F32, name="res%d" % v)
+            nc.scalar.activation(root[:], den[v][:], ACT.Abs_reciprocal_sqrt, bias=HALF)
+            nc.scalar.activation(rec[:], root[:], ACT.Square)
+            nc.vector.tensor_tensor(res[:], top[:, :, narrow[v]], rec[:], ALU.mult)
+            nc.sync.dma_start(out=out_rows[:, :, narrow[v]], in_=res[:])
+            quantise_out(weave_out(res, "woven%d" % v, False), narrow[v])
         for r in range(4):
-            (nc.scalar if r % 2 else nc.sync).dma_start(out=sc_rows[r:16:4, :], in_=o_sc[:].bitcast(I32)[r:P:32, :])
+            queue = nc.scalar if r % 2 else nc.sync
+            queue.dma_start(out=out_2[0].bitcast(I32)[r:BLOCKS:4, :], in_=o_sc[:].bitcast(I32)[r:P:32, :])

@@ -252,7 +252,7 @@ def tile_picked_hmixgvarnorm2_none_po_kernel(
         den_ps = [bank(u, [P, turns, P], "den_ps%d" % u) for u in range(2)]
         rec_ps = [bank(2 + u, [P, turns, P], "rec_ps%d" % u) for u in range(2)]
         for u in range(2):
-            other = keep.tile([P, 2, wide], F32, name="other_wide%d" % u)
+            other = keep.tile([P, 2, wide], F32, name="other_wide%d" % u, tag="other%d" % u)
             gather_other(other, (2 * u, 2 * u + 1), 0, wide)
             for b in range(turns):
                 own = h_abs[:, 2 * u + b // 2, (b % 2) * P : (b % 2 + 1) * P]
@@ -263,24 +263,20 @@ def tile_picked_hmixgvarnorm2_none_po_kernel(
         rec_wide = [keep.tile([P, turns * P], F32, name="rec_wide%d" % u, tag="rec_wide%d" % u) for u in range(2)]
         for u in range(2):
             nc.scalar.activation(root_wide[:, u, :], den_ps[u][:].rearrange("p b j -> p (b j)"), ACT.Abs_reciprocal_sqrt, bias=HALF)
-            nc.scalar.activation(rec_wide[u][:], root_wide[:, u, :], ACT.Square)
+            nc.gpsimd.tensor_tensor(rec_wide[u][:], root_wide[:, u, :], root_wide[:, u, :], ALU.mult)
             for b in range(turns):
                 nc.tensor.transpose(rec_ps[u][:, b, :], rec_wide[u][:, b * P : (b + 1) * P], ident[:])
+        narrow = [slice(wide + v * CHUNK, wide + (v + 1) * CHUNK) for v in range(2)]
+        other_narrow = [keep.tile([P, PLANES, CHUNK], F32, name="other_narrow%d" % v, tag="other%d" % v) for v in range(2)]
+        den = [keep.tile([P, PLANES, CHUNK], F32, name="den%d" % v) for v in range(2)]
         for u in range(2):
+            gather_other(other_narrow[u], range(PLANES), narrow[u].start, CHUNK)
+            nc.vector.tensor_tensor(den[u][:], h_abs[:, :, narrow[u]], other_narrow[u][:], ALU.add)
             planes = slice(2 * u, 2 * u + 2)
             nc.vector.tensor_tensor(res_wide[:, planes, :], top[:, planes, wide_cols],
                                     rec_ps[u][:].rearrange("p (t c) j -> p t (c j)", t=2), ALU.mult)
             nc.sync.dma_start(out=out_rows[:, planes, wide_cols], in_=res_wide[:, planes, :])
-
-        narrow = [slice(wide + v * CHUNK, wide + (v + 1) * CHUNK) for v in range(2)]
-        other_narrow = keep.tile([P, 2, PLANES, CHUNK], F32, name="other_narrow", tag="root_wide")
-        den = [keep.tile([P, PLANES, CHUNK], F32, name="den%d" % v, tag="rec_wide%d" % (1 - v)) for v in range(2)]
-        for v in range(2):
-            gather_other(other_narrow[:, v], range(PLANES), narrow[v].start, CHUNK)
-        nc.vector.tensor_tensor(den[0][:], h_abs[:, :, narrow[0]], other_narrow[:, 0], ALU.add)
-        woven_wide = weave_out(res_wide, "woven_wide", False)
-        nc.vector.tensor_tensor(den[1][:], h_abs[:, :, narrow[1]], other_narrow[:, 1], ALU.add)
-        quantise_out(woven_wide, wide_cols)
+        quantise_out(weave_out(res_wide, "woven_wide", False), wide_cols)
         for v in range(2):
             root = keep.tile([P, PLANES, CHUNK], F32, name="root%d" % v)
             rec = keep.tile([P, PLANES, CHUNK], F32, name="rec%d" % v)

from contextlib import ExitStack

import concourse.mybir as mybir
from concourse.masks import make_identity

F32 = mybir.dt.float32
BF16 = mybir.dt.bfloat16
I32 = mybir.dt.int32
U32 = mybir.dt.uint32
U16 = mybir.dt.uint16
U8 = mybir.dt.uint8
FP8X4 = mybir.dt.float8_e4m3fn_x4
ALU = mybir.AluOpType
ACT = mybir.ActivationFunctionType

P = 128
PLANES = 4
BLOCKS = 16
T = 2048
S = 512
MEMBERS = 4
LIST_ROWS = 16
SPARE = 16
CHUNK = 128
HALF = 0.5
FLOPS = 3 * 2 * 512 * 512 * 512

GROUPS = ((0, 128), (128, 128), (256, 128), (384, 64), (448, 64))
GATHERS = ((0, 0), (1, 0), (0, 1), (0, 2), (0, 3), (1, 1), (1, 2), (1, 3)) + tuple((g, t) for g in (2, 3, 4) for t in range(PLANES))


def words_view(dram):
    return dram[0].rearrange("p n t -> p (n t)").bitcast(I32)


def deal(engine, dealt, raw):
    engine.tensor_copy(out=dealt.rearrange("p (t m) -> p t m", t=PLANES), in_=raw.rearrange("p (m t) -> p t m", t=PLANES))


def weave(nc, woven, planes):
    nc.vector.tensor_copy(
        out=woven.rearrange("p (c i t) -> p c t i", i=4, t=PLANES),
        in_=planes.rearrange("p t (c i) -> p c t i", i=4),
    )


def entries(first, count):
    return slice(first // LIST_ROWS, (first + count) // LIST_ROWS)


def tile_picked_hmixgvarnorm2_none_po_kernel(
    tc, x_words, x_scales, w1_words, w1_scales, gn, w2_words, w2_scales, w3_words, w3_scales,
    offs, n1, two, n2, n3, out_0, out_1, out_2,
):
    nc = tc.nc
    with ExitStack() as ctx:
        keep = ctx.enter_context(tc.tile_pool(name="keep", bufs=1))
        ring = ctx.enter_context(tc.tile_pool(name="ring", bufs=3))
        psum = ctx.enter_context(tc.psum_pool(name="psum", bufs=1))

        def load_list(dram, name):
            tile = keep.tile(list(dram.shape), U16, name=name)
            nc.sync.dma_start(tile[:], dram)
            return tile

        def bank(b, shape, name):
            return psum.tile(shape, F32, name=name, tag="bank%d" % b)

        xq_sc = keep.tile([P, S], U8, name="xq_sc", align_bytes=64)
        x2_sc = keep.tile([P, S], U8, name="x2_sc", align_bytes=64)
        nc.vector.memset(xq_sc[:].bitcast(I32), 0)
        nc.vector.memset(x2_sc[:].bitcast(I32), 0)
        ysq = [keep.tile([P, S + SPARE], F32, name="ysq%d" % t) for t in range(PLANES)]
        for t in range(PLANES):
            nc.vector.memset(ysq[t][:, S:], 0.0)
        warm_in = keep.tile([P, 1], F32, name="warm_in")
        warm_out = keep.tile([P, 1], F32, name="warm_out")
        nc.vector.memset(warm_in[:], 1.0)
        nc.scalar.activation(warm_out[:], warm_in[:], ACT.Abs_reciprocal_sqrt)
        ident = keep.tile([P, P], F32, name="ident")
        make_identity(nc, ident[:])

        xs = keep.tile([P, T], U8, name="xs")
        nc.sync.dma_start(out=xs[:].bitcast(I32), in_=x_scales[0].bitcast(I32).unsqueeze(1).broadcast_to([BLOCKS, P // BLOCKS, T // 4]))
        offs_t = load_list(offs, "offs_t")
        xw = keep.tile([P, T], U32, name="xw")
        nc.sync.dma_start(out=xw[:].bitcast(I32), in_=words_view(x_words))
        w_raw = keep.tile([P, S], I32, name="w_raw")
        nc.sync.dma_start(out=w_raw[:], in_=words_view(w1_words))
        w_sc_raw = keep.tile([P, S], U8, name="w_sc_raw")
        for q in range(4):
            rows = w1_scales[0].bitcast(I32)[4 * q : 4 * q + 4, :]
            nc.scalar.dma_start(out=w_sc_raw[:].bitcast(I32)[32 * q : 32 * q + 32, :], in_=rows.unsqueeze(0).broadcast_to([8, 4, S // 4]))
        n1_t = load_list(n1, "n1_t")
        two_t = load_list(two, "two_t")
        gain = keep.tile([P, PLANES], F32, name="gain")
        nc.gpsimd.dma_start(out=gain[:], in_=gn.rearrange("(p t) o -> p (t o)", t=PLANES))

        def pick_scales(offsets, plane, name, tag, queues):
            picked = keep.tile([P, S], U8, name=name, tag=tag, align_bytes=64)
            nc.vector.tensor_copy(picked[:], xs[:].indirect(offsets[:]))
            for r in range(4):
                queues[r % len(queues)].dma_start(out=plane[:].bitcast(I32)[r:P:32, :], in_=picked[:].bitcast(I32)[8 * r : P : 32, :])

        pick_scales(offs_t, xq_sc, "xq_picked", "xq_picked", (nc.scalar, nc.sync))
        w1_sc = keep.tile([P, S], U8, name="w1_sc", align_bytes=64)
        deal(nc.vector, w1_sc[:], w_sc_raw[:])
        xq = keep.tile([P, S], U32, name="xq", align_bytes=64)
        nc.vector.tensor_copy(xq[:], xw[:].indirect(offs_t[:]))
        w1 = keep.tile([P, S], I32, name="w1", align_bytes=64)
        deal(nc.vector, w1[:], w_raw[:])

        y_ps = [bank(t, [P, S], "y_ps%d" % t) for t in range(PLANES)]
        for t in range(PLANES):
            cols = slice(t * P, (t + 1) * P)
            nc.tensor.matmul_mx(y_ps[t][:], lhsT=w1[:, cols].bitcast(FP8X4), lhsT_scale=w1_sc[:, cols],
                                rhs=xq[:].bitcast(FP8X4), rhs_scale=xq_sc[:], start=True, stop=True)
        nc.scalar.activation(ysq[0][:, :S], y_ps[0][:], ACT.Square)
        for t in range(1, PLANES):
            y_copy = keep.tile([P, S], F32, name="y_copy%d" % t, tag="y_copy%d" % t, align_bytes=64)
            nc.vector.tensor_copy(y_copy[:], y_ps[t][:])
            nc.vector.tensor_tensor(ysq[t][:, :S], y_ps[t][:], y_copy[:], ALU.mult)

        n3_t = load_list(n3, "n3_t")
        n2_t = load_list(n2, "n2_t")
        w2 = keep.tile([P, S], I32, name="w2", align_bytes=64)
        w3 = keep.tile([P, S], I32, name="w3", tag="y_copy2", align_bytes=64)
        w23_sc = keep.tile([P, S], U8, name="w23_sc", align_bytes=64)
        nc.sync.dma_start(out=w_raw[:], in_=words_view(w3_words))
        for first, scales in ((0, w2_scales), (4, w3_scales)):
            for r in range(4):
                nc.sync.dma_start(out=w_sc_raw[:].bitcast(I32)[first + r : P : 32, :], in_=scales[0].bitcast(I32)[r:BLOCKS:4, :])
        x2 = keep.tile([P, S], U32, name="x2", align_bytes=64)
        nc.vector.tensor_copy(x2[:], xw[:].indirect(two_t[:]))
        pick_scales(two_t, x2_sc, "x2_picked", "y_copy3", (nc.sync,))
        deal(nc.vector, w3[:], w_raw[:])
        nc.sync.dma_start(out=w_raw[:], in_=words_view(w2_words))
        deal(nc.vector, w23_sc[:], w_sc_raw[:])
        deal(nc.vector, w2[:], w_raw[:])

        qs = keep.tile([P, PLANES, S], F32, name="qs")
        rs = keep.tile([P, PLANES, S], F32, name="rs")
        zb = keep.tile([P, PLANES, S], BF16, name="zb")
        z_woven = keep.tile([P, S * PLANES], BF16, name="z_woven", align_bytes=64)
        zq = keep.tile([P, S], U32, name="zq", align_bytes=64)
        z_sc = keep.tile([P, S], U8, name="z_sc", align_bytes=64)
        h_both = keep.tile([P, 2 * PLANES * S], F32, name="h_both")
        h = h_both[:, : PLANES * S].rearrange("p (t j) -> p t j", t=PLANES)
        h_abs = h_both[:, PLANES * S :].rearrange("p (t j) -> p t j", t=PLANES)
        chunks = S // CHUNK
        h_ps = [[bank(PLANES + 2 * (c % 2) + u, [P, 2, CHUNK], "h_ps%d_%d" % (c, u)) for u in range(2)] for c in range(chunks)]
        last_group = len(GROUPS) - 1
        last_cols = slice(S - CHUNK, S)

        def sums(g):
            first, width = GROUPS[g]
            return h_abs[:, :, :width] if g == last_group else qs[:, :, first : first + width]

        def h_pass(c, weights, plane_row, codes, scales, opens):
            cols = slice(c * CHUNK, (c + 1) * CHUNK)
            for t in range(PLANES):
                w_cols = slice(t * P, (t + 1) * P)
                nc.tensor.matmul_mx(h_ps[c][t // 2][:, t % 2, :], lhsT=weights[:, w_cols].bitcast(FP8X4), lhsT_scale=w23_sc[plane_row:P, w_cols],
                                    rhs=codes[:, cols].bitcast(FP8X4), rhs_scale=scales[:, cols],
                                    start=opens and t % 2 == 0, stop=not opens and t % 2 == 1)

        def gather_members(g, t):
            first, width = GROUPS[g]
            n = width * MEMBERS
            members = ring.tile([P, CHUNK * MEMBERS], F32, name="members")
            nc.scalar.activation(members[:, :n], ysq[t][:].indirect(n1_t[:, entries(first * MEMBERS, n)]), ACT.Copy)
            nc.vector.tensor_reduce(sums(g)[:, t, :], members[:, :n].rearrange("p (j m) -> p j m", m=MEMBERS),
                                    axis=mybir.AxisListType.X, op=ALU.add)

        def scale_z(g):
            first, width = GROUPS[g]
            cols = slice(first, first + width)
            for t0, t1 in ((0, PLANES - 1), (PLANES - 1, PLANES)) if g == last_group else ((0, PLANES),):
                nc.scalar.activation(rs[:, t0:t1, cols], sums(g)[:, t0:t1, :], ACT.Abs_reciprocal_sqrt, bias=HALF)
                for t in range(t0, t1):
                    nc.vector.scalar_tensor_tensor(zb[:, t, cols], y_ps[t][:, cols], gain[:, t : t + 1], rs[:, t, cols], ALU.mult, ALU.mult)

        def quantise_z(g):
            first, width = GROUPS[g]
            cols = slice(first, first + width)
            woven = z_woven[:, first * PLANES : (first + width) * PLANES]
            weave(nc, woven, zb[:, :, cols])
            nc.vector.quantize_mx(zq[:, cols].bitcast(FP8X4), z_sc[:, cols], woven)
            if (first + width) % CHUNK == 0:
                h_pass(first // CHUNK, w2, 0, zq, z_sc, False)

        def copy_h(c):
            for u in range(2):
                nc.vector.tensor_copy(h[:, 2 * u : 2 * u + 2, c * CHUNK : (c + 1) * CHUNK], h_ps[c][u][:])
            if c + 2 < chunks:
                h_pass(c + 2, w3, 4, x2, x2_sc, True)

        h_pass(0, w3, 4, x2, x2_sc, True)
        h_pass(1, w3, 4, x2, x2_sc, True)
        summed = None
        age = 0
        for g, t in GATHERS:
            gather_members(g, t)
            if summed is not None:
                age = age + 1
                if age == 1:
                    scale_z(summed)
                if age == 2:
                    quantise_z(summed)
                if age == 3 and summed < chunks - 1:
                    copy_h(summed)
            if t == PLANES - 1:
                summed = g
                age = 0
        scale_z(last_group)
        quantise_z(last_group)
        nc.scalar.activation(h_abs[:, :, : S - CHUNK], h[:, :, : S - CHUNK], ACT.Abs)
        for u in range(2):
            nc.scalar.activation(h_abs[:, 2 * u : 2 * u + 2, last_cols], h_ps[-1][u][:], ACT.Abs)
            nc.vector.tensor_copy(h[:, 2 - 2 * u : 4 - 2 * u, last_cols], h_ps[-1][1 - u][:])

        o_words = keep.tile([P, S], U32, name="o_words", align_bytes=64)
        o_sc = keep.tile([P, S], U8, name="o_sc", align_bytes=64)
        out_rows = out_0.rearrange("(p t) j -> p t j", t=PLANES)
        out_words = words_view(out_1)
        top = keep.tile([P, PLANES, S], F32, name="top")
        for t in range(PLANES):
            nc.vector.tensor_copy(top[:, t, :], h_both[:, t * S : (t + 2) * S].indirect(n2_t[:]))

        def gather_other(other, planes, first, width):
            for i, t in enumerate(planes):
                nc.scalar.activation(other[:, i, :], h_abs[:, t, :].indirect(n3_t[:, entries(first, width)]), ACT.Copy)

        def weave_out(res, name, on_gpsimd):
            woven = keep.tile([P, PLANES * res.shape[2]], BF16, name=name, align_bytes=64)
            if on_gpsimd:
                nc.gpsimd.tensor_scalar(woven[:].rearrange("p (c i t) -> p c t i", i=4, t=PLANES), res[:].rearrange("p t (c i) -> p c t i", i=4),
                                        1.0, 0.0, ALU.mult, ALU.add)
            else:
                weave(nc, woven[:], res[:])
            return woven

        def quantise_out(woven, cols):
            nc.vector.quantize_mx(o_words[:, cols].bitcast(FP8X4), o_sc[:, cols], woven[:])
            nc.sync.dma_start(out=out_words[:, cols], in_=o_words[:, cols].bitcast(I32))

        wide = S // 2
        wide_cols = slice(0, wide)
        turns = 2 * wide // P
        root_wide = keep.tile([P, 2, 2 * wide], F32, name="root_wide", tag="root_wide")
        res_wide = keep.tile([P, PLANES, wide], F32, name="res_wide")
        den_ps = [bank(u, [P, turns, P], "den_ps%d" % u) for u in range(2)]
        rec_ps = [bank(2 + u, [P, turns, P], "rec_ps%d" % u) for u in range(2)]
        for u in range(2):
            other = keep.tile([P, 2, wide], F32, name="other_wide%d" % u, tag="other%d" % u)
            gather_other(other, (2 * u, 2 * u + 1), 0, wide)
            for b in range(turns):
                own = h_abs[:, 2 * u + b // 2, (b % 2) * P : (b % 2 + 1) * P]
                nc.tensor.matmul(den_ps[u][:, b, :], lhsT=own, rhs=ident[:], is_transpose=True, start=b == 0, stop=False)
            for b in range(turns):
                nc.tensor.matmul(den_ps[u][:, b, :], lhsT=other[:, b // 2, (b % 2) * P : (b % 2 + 1) * P], rhs=ident[:],
                                 is_transpose=True, start=False, stop=b == turns - 1)
        rec_wide = [keep.tile([P, turns * P], F32, name="rec_wide%d" % u, tag="rec_wide%d" % u) for u in range(2)]
        for u in range(2):
            nc.scalar.activation(root_wide[:, u, :], den_ps[u][:].rearrange("p b j -> p (b j)"), ACT.Abs_reciprocal_sqrt, bias=HALF)
            nc.gpsimd.tensor_tensor(rec_wide[u][:], root_wide[:, u, :], root_wide[:, u, :], ALU.mult)
            for b in range(turns):
                nc.tensor.transpose(rec_ps[u][:, b, :], rec_wide[u][:, b * P : (b + 1) * P], ident[:])
        narrow = [slice(wide + v * CHUNK, wide + (v + 1) * CHUNK) for v in range(2)]
        other_narrow = [keep.tile([P, PLANES, CHUNK], F32, name="other_narrow%d" % v, tag="other%d" % v) for v in range(2)]
        den = [keep.tile([P, PLANES, CHUNK], F32, name="den%d" % v) for v in range(2)]
        for u in range(2):
            gather_other(other_narrow[u], range(PLANES), narrow[u].start, CHUNK)
            nc.vector.tensor_tensor(den[u][:], h_abs[:, :, narrow[u]], other_narrow[u][:], ALU.add)
            planes = slice(2 * u, 2 * u + 2)
            nc.vector.tensor_tensor(res_wide[:, planes, :], top[:, planes, wide_cols],
                                    rec_ps[u][:].rearrange("p (t c) j -> p t (c j)", t=2), ALU.mult)
            nc.sync.dma_start(out=out_rows[:, planes, wide_cols], in_=res_wide[:, planes, :])
        quantise_out(weave_out(res_wide, "woven_wide", False), wide_cols)
        for v in range(2):
            root = keep.tile([P, PLANES, CHUNK], F32, name="root%d" % v)
            rec = keep.tile([P, PLANES, CHUNK], F32, name="rec%d" % v)
            res = keep.tile([P, PLANES, CHUNK], F32, name="res%d" % v)
            nc.scalar.activation(root[:], den[v][:], ACT.Abs_reciprocal_sqrt, bias=HALF)
            nc.scalar.activation(rec[:], root[:], ACT.Square)
            nc.vector.tensor_tensor(res[:], top[:, :, narrow[v]], rec[:], ALU.mult)
            nc.sync.dma_start(out=out_rows[:, :, narrow[v]], in_=res[:])
            quantise_out(weave_out(res, "woven%d" % v, False), narrow[v])
        for r in range(4):
            queue = nc.scalar if r % 2 else nc.sync
            queue.dma_start(out=out_2[0].bitcast(I32)[r:BLOCKS:4, :], in_=o_sc[:].bitcast(I32)[r:P:32, :])
